import numpy as np
import ml_dtypes


def mxq(x, axis, fmt="e4m3"):
    dtype, down = {"e4m3": (ml_dtypes.float8_e4m3fn, 7), "e5m2": (ml_dtypes.float8_e5m2, 14)}[fmt]
    v = np.moveaxis(np.asarray(x, np.float32).astype(ml_dtypes.bfloat16).astype(np.float64), axis, -1)
    blocks = v.reshape(v.shape[:-1] + (-1, 32))
    amax = np.abs(blocks).max(-1, keepdims=True)
    byte = np.maximum(np.where(amax > 0, np.frexp(amax)[1] - 1 + 127, 0) - down, 1)
    scale = np.exp2(byte - 127.0)
    codes = (blocks / scale).astype(np.float32).astype(dtype).astype(np.float64)
    return np.moveaxis((codes * scale).reshape(v.shape), -1, axis)


WIDE = False


def mx_kscale(k):
    if not WIDE:
        return np.ones(k)
    levels = np.array([10, -10, 5, -5, 0])
    if k % 512:
        return np.exp2(np.random.permutation(np.resize(levels, k // 32))).repeat(32)
    a = np.empty((k // 512, 16))
    for p in range(k // 512):
        a[p, :8] = np.random.permutation(np.resize(levels, 8))
        for g in range(8):
            far = levels[np.abs(levels - a[p, g]) >= 10]
            a[p, g + 8] = far[np.random.randint(len(far))]
    return np.exp2(a.ravel()).repeat(32)


def f64(x):
    return np.asarray(x).astype(np.float64)


def striped(idx):
    return np.tile(idx.reshape(-1, 16).T, (8, 1)).astype(np.uint16)


def unstriped(offs):
    return offs[:16].T.reshape(-1).astype(np.int64)


def striped8(idx):
    return np.concatenate([x.reshape(-1, 16).T for x in idx]).astype(np.uint16)


def runs(offs, k):
    lists = np.stack([offs[16 * r : 16 * r + 16].T.reshape(-1) for r in range(8)]).astype(np.int64)
    return lists[np.arange(k) % 512 // 64]


def pack_weight(w):
    k, n = w.shape
    w = f64(np.asarray(w, np.float32).astype(ml_dtypes.bfloat16)).reshape(k // 32, 32, n)
    amax = np.abs(w).max(1)
    byte = np.clip(np.where(amax > 0, np.frexp(amax)[1] - 1 + 127 - 7, 1), 1, 254)
    scaled = (w * np.exp2(127.0 - byte)[:, None, :]).reshape(k, n).astype(np.float32)
    words = np.ascontiguousarray(scaled.reshape(k // 512, 128, 4, n).transpose(0, 1, 3, 2)).astype(ml_dtypes.float8_e4m3fn).view(np.uint8)
    return words, np.ascontiguousarray(byte.astype(np.uint8).reshape(k // 512, 16, n))


def unpack_weight(words, scales):
    g, p, n, _ = words.shape
    vals = np.ascontiguousarray(words).view(ml_dtypes.float8_e4m3fn).astype(np.float64) * np.repeat(np.exp2(scales.astype(np.float64) - 127.0), 8, axis=1)[..., None]
    return vals.transpose(0, 1, 3, 2).reshape(g * 512, n)

def planes(y):
    n, m = y.shape
    v = y.astype(np.float32).astype(ml_dtypes.bfloat16).astype(np.float64).reshape(n // 32, 32, m)
    top = np.abs(v).max(1)
    byte = np.clip(np.where(top > 0, np.frexp(top)[1] - 1 + 127 - 7, 1), 1, 254)
    codes = (v * np.exp2(127.0 - byte)[:, None, :]).reshape(n, m).astype(np.float32).astype(ml_dtypes.float8_e4m3fn).view(np.uint8)
    words = codes.reshape(n // 512, 128, 4, m).transpose(0, 1, 3, 2)
    return np.ascontiguousarray(words), np.ascontiguousarray(byte.astype(np.uint8).reshape(n // 512, 16, m))


K, T, S, N, G, H = 512, 2048, 512, 512, 2048, 512


def setup_inputs():
    n = np.random.standard_normal
    s = mx_kscale(K)[:, None]
    u = mx_kscale(S)
    packed_xT = pack_weight(n((K, T)) * s)
    packed_dT = pack_weight(n((K, G)) / s)
    packed_w1 = pack_weight(n((H, N)) / np.sqrt(H) / u[:, None])
    return {
        "x_words": packed_xT[0],
        "x_scales": packed_xT[1],
        "d_words": packed_dT[0],
        "d_scales": packed_dT[1],
        "gn": (np.random.uniform(0.5, 1.5, (H, 1)) * u[:, None]).astype(np.float32),
        "w1_words": packed_w1[0],
        "w1_scales": packed_w1[1],
        "offs": striped8(np.random.randint(0, T, (8, S))),
        "k1": striped8(np.random.randint(0, G, (8, H))),
        "n1": striped(np.random.randint(0, S, G)),
        "n2": striped(np.random.permutation(S)),
        "n3": striped(np.random.permutation(S)),
    }


def reference(x_words, x_scales, d_words, d_scales, gn, w1_words, w1_scales, offs, k1, n1, n2, n3):
    d_k1 = unpack_weight(d_words, d_scales)[np.arange(K)[:, None], runs(k1, K)]
    xq = unpack_weight(x_words, x_scales)[np.arange(K)[:, None], runs(offs, K)]
    h = 0.0625 * (d_k1.T @ xq)
    mb = h[:, unstriped(n1)]
    mx = mb.reshape(H, S, 4).max(axis=2)
    mn = mb.reshape(H, S, 4).min(axis=2)
    z = f64(gn) * (mx - (0.5 * mn))
    h2 = unpack_weight(w1_words, w1_scales).T @ mxq(z, 0, "e4m3")
    out_0 = h2[:, unstriped(n2)] - h2[:, unstriped(n3)]
    return (out_0,) + planes(out_0)

@@ -1,0 +1,283 @@
+from contextlib import ExitStack
+
+import concourse.mybir as mybir
+
+K, T, S, N, G, H = 512, 2048, 512, 512, 2048, 512
+FLOPS = 2 * K * H * S + 2 * H * N * S
+
+F32 = mybir.dt.float32
+BF16 = mybir.dt.bfloat16
+I32 = mybir.dt.int32
+U32 = mybir.dt.uint32
+U16 = mybir.dt.uint16
+U8 = mybir.dt.uint8
+FP8X4 = mybir.dt.float8_e4m3fn_x4
+ALU = mybir.AluOpType
+ACT = mybir.ActivationFunctionType
+
+P = 128
+PACK = 4
+MEMBERS = 4
+HALF = 256
+CHUNK = 128
+UNIT = 64
+VECTOR_FETCHES = 2
+
+
+def as_words(packed):
+    return packed[0].rearrange("p n t -> p (n t)").bitcast(I32)
+
+
+def entries(list_tile, first, count):
+    return list_tile[:, first // 16 : (first + count) // 16]
+
+
+def tile_picked_hpqgspangap_none_po_kernel(
+    tc, x_words, x_scales, d_words, d_scales, gn, w1_words, w1_scales, offs, k1, n1, n2, n3, out_0, out_1, out_2
+):
+    nc = tc.nc
+    chunks = S // CHUNK
+    with ExitStack() as ctx:
+        lists = ctx.enter_context(tc.tile_pool(name="lists", bufs=1))
+        keep = ctx.enter_context(tc.tile_pool(name="keep", bufs=1))
+        psum = ctx.enter_context(tc.psum_pool(name="psum", bufs=1))
+
+        k1_list = lists.tile([P, H // 16], U16, name="k1_list")
+        offs_list = lists.tile([P, S // 16], U16, name="offs_list")
+        n1_list = lists.tile([P, G // 16], U16, name="n1_list")
+        n2_list = lists.tile([P, S // 16], U16, name="n2_list")
+        n3_list = lists.tile([P, S // 16], U16, name="n3_list")
+
+        d_word_table = keep.tile([P, G], I32, name="d_word_table")
+        x_word_table = keep.tile([P, T], I32, name="x_word_table")
+        d_byte_table = keep.tile([P, G], U8, name="d_byte_table")
+        x_byte_table = keep.tile([P, T], U8, name="x_byte_table")
+        w1_raw_words = keep.tile([P, N], I32, name="w1_raw_words")
+        w1_raw_bytes = keep.tile([P, N], U8, name="w1_raw_bytes")
+        gain = keep.tile([P, PACK], F32, name="gain")
+        plane = keep.tile([P, S + H], U8, name="plane", align_bytes=64)
+
+        nc.gpsimd.memset(d_byte_table[:].bitcast(I32), 0)
+        nc.vector.memset(x_byte_table[:].bitcast(I32), 0)
+        nc.sync.dma_start(k1_list[:], k1)
+        nc.sync.dma_start(offs_list[:], offs)
+        nc.sync.dma_start(n1_list[:], n1)
+        nc.sync.dma_start(n2_list[:], n2)
+        nc.sync.dma_start(n3_list[:], n3)
+        nc.sync.dma_start(d_byte_table[:].bitcast(I32)[0:P:8, :], d_scales[0].bitcast(I32))
+        nc.sync.dma_start(x_byte_table[:].bitcast(I32)[0:P:8, :], x_scales[0].bitcast(I32))
+        nc.sync.dma_start(d_word_table[:], as_words(d_words))
+        nc.sync.dma_start(x_word_table[:], as_words(x_words))
+        nc.sync.dma_start(w1_raw_words[:], as_words(w1_words))
+
+        nc.gpsimd.dma_start(gain[:], gn.rearrange("(p t) o -> p (t o)", t=PACK))
+        nc.gpsimd.memset(plane[:].bitcast(I32), 0)
+        nc.gpsimd.memset(w1_raw_bytes[:].bitcast(I32), 0)
+        for q in range(4):
+            nc.gpsimd.dma_start(
+                w1_raw_bytes[:].bitcast(I32)[32 * q : 32 * q + 4, :], w1_scales[0].bitcast(I32)[4 * q : 4 * q + 4, :]
+            )
+
+        gain_size = keep.tile([P, PACK], F32, name="gain_size")
+        gain_sign = keep.tile([P, CHUNK, PACK], BF16, name="gain_sign")
+        nc.scalar.activation(gain_size[:], gain[:], ACT.Abs, scale=0.0625)
+        nc.scalar.activation(gain_sign[:], gain[:].unsqueeze(1).broadcast_to([P, CHUNK, PACK]), ACT.Sign)
+
+        d_picked_bytes = keep.tile([P, H], U8, name="d_picked_bytes")
+        x_picked_bytes = keep.tile([P, S], U8, name="x_picked_bytes")
+        staged_bytes = keep.tile([P, S + H], U8, name="staged_bytes")
+        nc.vector.tensor_copy(d_picked_bytes[:], d_byte_table[:].indirect(k1_list[:]))
+        nc.vector.tensor_copy(
+            staged_bytes[:, S:].rearrange("p (t m) -> p t m", t=PACK),
+            d_picked_bytes[:].rearrange("p (m t) -> p t m", t=PACK),
+        )
+        nc.vector.tensor_copy(x_picked_bytes[:], x_byte_table[:].indirect(offs_list[:]))
+        nc.vector.tensor_copy(staged_bytes[:].bitcast(I32)[:, : S // 4], x_picked_bytes[:].bitcast(I32))
+        for c in range(4):
+            nc.scalar.dma_start(plane[:].bitcast(I32)[c:P:32, :], staged_bytes[:].bitcast(I32)[8 * c : P : 32, :])
+
+        d_picked_words = keep.tile([P, H], U32, name="d_picked_words")
+        d_dealt_words = keep.tile([P, H], U32, name="d_dealt_words", align_bytes=64)
+        nc.vector.tensor_copy(d_picked_words[:], d_word_table[:].bitcast(U32).indirect(k1_list[:]))
+        nc.vector.tensor_copy(
+            d_dealt_words[:].bitcast(I32).rearrange("p (t m) -> p t m", t=PACK),
+            d_picked_words[:].bitcast(I32).rearrange("p (m t) -> p t m", t=PACK),
+        )
+
+        h_rows = [keep.tile([P, S], F32, name=f"h_rows{t}") for t in range(PACK)]
+        for half in range(S // HALF):
+            cols = slice(half * HALF, (half + 1) * HALF)
+            x_picked_words = keep.tile([P, HALF], U32, name=f"x_picked_words{half}", align_bytes=64)
+            nc.vector.tensor_copy(
+                x_picked_words[:], x_word_table[:].bitcast(U32).indirect(entries(offs_list, cols.start, HALF))
+            )
+            for t in range(PACK):
+                bank = psum.tile([P, HALF], F32, name=f"h_bank{half}_{t}", tag=f"bank{PACK * half + t}")
+                nc.tensor.matmul_mx(
+                    out=bank[:],
+                    lhsT=d_dealt_words[:, t * P : (t + 1) * P].bitcast(FP8X4),
+                    lhsT_scale=plane[:, S + t * P : S + (t + 1) * P],
+                    rhs=x_picked_words[:].bitcast(FP8X4),
+                    rhs_scale=plane[:, cols],
+                    start=True,
+                    stop=True,
+                )
+                if half == 0 or t == 0:
+                    nc.scalar.activation(h_rows[t][:, cols], bank[:], ACT.Copy, scale=gain_size[:, t : t + 1])
+                else:
+                    nc.vector.tensor_scalar(h_rows[t][:, cols], bank[:], gain_size[:, t : t + 1], None, ALU.mult)
+
+        w1_dealt_words = keep.tile([P, N], I32, name="w1_dealt_words", align_bytes=64)
+        w1_dealt_bytes = keep.tile([P, N], U8, name="w1_dealt_bytes", align_bytes=64)
+        nc.gpsimd.tensor_copy(
+            w1_dealt_bytes[:].rearrange("p (t m) -> p t m", t=PACK),
+            w1_raw_bytes[:].rearrange("p (m t) -> p t m", t=PACK),
+        )
+        nc.gpsimd.tensor_copy(
+            w1_dealt_words[:].rearrange("p (t m) -> p t m", t=PACK),
+            w1_raw_words[:].rearrange("p (m t) -> p t m", t=PACK),
+        )
+
+        units = S // UNIT
+        members = [keep.tile([P, PACK, UNIT * MEMBERS], F32, name=f"members{u}") for u in range(units)]
+        for u in range(units):
+            for t in range(PACK):
+                looked_up = h_rows[t][:].indirect(entries(n1_list, u * UNIT * MEMBERS, UNIT * MEMBERS))
+                if u < VECTOR_FETCHES and t == PACK - 1:
+                    nc.vector.tensor_copy(members[u][:, t, :], looked_up)
+                else:
+                    nc.scalar.activation(members[u][:, t, :], looked_up, ACT.Copy)
+
+        h2_rows = [keep.tile([P, S], F32, name=f"h2_rows{t}") for t in range(PACK)]
+        early = (chunks - 1) * CHUNK
+        early_banks = [psum.tile([P, early], F32, name=f"h2_early{t}", tag=f"bank{t}") for t in range(PACK)]
+        late_banks = [psum.tile([P, CHUNK], F32, name=f"h2_late{t}", tag=f"bank{PACK + t}") for t in range(PACK)]
+
+        larger = keep.tile([P, S, PACK, 2], F32, name="larger")
+        smaller = keep.tile([P, S, PACK, 2], F32, name="smaller")
+        largest = keep.tile([P, S * PACK], F32, name="largest")
+        smallest = keep.tile([P, S * PACK], F32, name="smallest")
+        z_size = keep.tile([P, S * PACK], BF16, name="z_size")
+        z = keep.tile([P, S * PACK], BF16, name="z", align_bytes=64)
+        z_words = keep.tile([P, S], U32, name="z_words", align_bytes=64)
+        z_bytes = keep.tile([P, S], U8, name="z_bytes", align_bytes=64)
+
+        def flat(cols):
+            return slice(cols.start * PACK, cols.stop * PACK)
+
+        def pair_level(u, op, pairs):
+            halves = members[u][:].rearrange("p t (j a e) -> p j t a e", a=2, e=2)
+            nc.vector.tensor_tensor(
+                pairs[:, u * UNIT : (u + 1) * UNIT, :, :], halves[:, :, :, 0, :], halves[:, :, :, 1, :], op
+            )
+
+        def last_level(cols, op, pairs, best):
+            both = pairs[:, cols, :, :].rearrange("p j t e -> p (j t) e")
+            nc.vector.tensor_tensor(best[:, flat(cols)], both[:, :, 0], both[:, :, 1], op)
+
+        def combine(cols):
+            nc.vector.scalar_tensor_tensor(
+                z_size[:, flat(cols)], smallest[:, flat(cols)], -0.5, largest[:, flat(cols)], ALU.mult, ALU.add
+            )
+
+        def give_sign(cols):
+            signs = gain_sign[:, : cols.stop - cols.start, :].rearrange("p j t -> p (j t)")
+            nc.vector.tensor_tensor(z[:, flat(cols)], z_size[:, flat(cols)], signs, ALU.mult)
+
+        def quantise(cols):
+            nc.vector.quantize_mx(out=z_words[:, cols].bitcast(FP8X4), scales=z_bytes[:, cols], in_=z[:, flat(cols)])
+
+        def second_product(cols, banks, bank_cols):
+            for t in range(PACK):
+                nc.tensor.matmul_mx(
+                    out=banks[t][:, bank_cols],
+                    lhsT=w1_dealt_words[:, t * P : (t + 1) * P].bitcast(FP8X4),
+                    lhsT_scale=w1_dealt_bytes[:, t * P : (t + 1) * P],
+                    rhs=z_words[:, cols].bitcast(FP8X4),
+                    rhs_scale=z_bytes[:, cols],
+                    start=True,
+                    stop=True,
+                )
+
+        for c in range(chunks):
+            first, second = 2 * c, 2 * c + 1
+            cols = slice(c * CHUNK, (c + 1) * CHUNK)
+            before = slice(cols.start - CHUNK, cols.start)
+            first_cols = slice(cols.start, cols.start + UNIT)
+            second_cols = slice(cols.start + UNIT, cols.stop)
+            last = c == chunks - 1
+            pair_level(first, ALU.max, larger)
+            if c > 0:
+                combine(before)
+            pair_level(first, ALU.min, smaller)
+            if c > 0:
+                give_sign(before)
+            if last:
+                last_level(first_cols, ALU.max, larger, largest)
+                quantise(before)
+                second_product(before, early_banks, before)
+                last_level(first_cols, ALU.min, smaller, smallest)
+                for t in range(PACK):
+                    nc.scalar.activation(h2_rows[t][:, :early], early_banks[t][:], ACT.Copy)
+                pair_level(second, ALU.max, larger)
+                pair_level(second, ALU.min, smaller)
+                last_level(second_cols, ALU.max, larger, largest)
+                last_level(second_cols, ALU.min, smaller, smallest)
+                for step in (combine, give_sign, quantise):
+                    step(first_cols)
+                    step(second_cols)
+                second_product(cols, late_banks, slice(0, CHUNK))
+            else:
+                pair_level(second, ALU.max, larger)
+                if c > 0:
+                    quantise(before)
+                    second_product(before, early_banks, before)
+                pair_level(second, ALU.min, smaller)
+                last_level(cols, ALU.max, larger, largest)
+                last_level(cols, ALU.min, smaller, smallest)
+        for t in range(PACK):
+            if t % 2 == 0:
+                nc.scalar.activation(h2_rows[t][:, early:], late_banks[t][:], ACT.Copy)
+            else:
+                nc.vector.tensor_copy(h2_rows[t][:, early:], late_banks[t][:])
+
+        out_rows = out_0.rearrange("(p t) j -> p t j", t=PACK)
+        y_bytes = keep.tile([P, S], U8, name="y_bytes", align_bytes=64)
+        taken = [keep.tile([P, PACK, HALF], F32, name=f"taken{half}") for half in range(S // HALF)]
+        for half in range(S // HALF):
+            for t in range(PACK):
+                nc.scalar.activation(
+                    taken[half][:, t, :], h2_rows[t][:].indirect(entries(n3_list, half * HALF, HALF)), ACT.Copy
+                )
+        ys = []
+        for half in range(S // HALF):
+            cols = slice(half * HALF, (half + 1) * HALF)
+            y = keep.tile([P, PACK, HALF], F32, name=f"y{half}")
+            for t in range(PACK):
+                nc.vector.tensor_tensor(
+                    y[:, t, :],
+                    h2_rows[t][:].indirect(entries(n2_list, cols.start, HALF)),
+                    taken[half][:, t, :],
+                    ALU.subtract,
+                )
+            nc.sync.dma_start(out_rows[:, :, cols], y[:])
+            ys.append(y)
+        for half in range(S // HALF):
+            cols = slice(half * HALF, (half + 1) * HALF)
+            y_rounded = keep.tile([P, HALF, PACK], BF16, name=f"y_rounded{half}", align_bytes=64)
+            src = ys[half][:].rearrange("p t (c i) -> p c t i", i=4)
+            dst = y_rounded[:].rearrange("p (c i) t -> p c t i", i=4)
+            if half == 0:
+                nc.scalar.copy(dst, src)
+            else:
+                nc.vector.tensor_copy(dst, src)
+            y_words = keep.tile([P, HALF], U32, name=f"y_words{half}", align_bytes=64)
+            nc.vector.quantize_mx(
+                out=y_words[:].bitcast(FP8X4), scales=y_bytes[:, cols], in_=y_rounded[:].rearrange("p j t -> p (j t)")
+            )
+            nc.sync.dma_start(as_words(out_1)[:, cols], y_words[:].bitcast(I32))
+        for q in range(4):
+            queue = nc.scalar if q % 2 == 0 else nc.sync
+            queue.dma_start(
+                out_2[0].bitcast(I32)[4 * q : 4 * q + 4, :], y_bytes[:].bitcast(I32)[32 * q : 32 * q + 4, :]
+            )

@@ -32,6 +32,16 @@ def entries(list_tile, first, count):
     return list_tile[:, first // 16 : (first + count) // 16]
 
 
+def deal_words(nc, dealt, raw):
+    nc.vector.tensor_copy(
+        dealt.rearrange("p (t c i) -> p c t i", t=PACK, i=4), raw.rearrange("p (c i t) -> p c t i", t=PACK, i=4)
+    )
+
+
+def deal_bytes(nc, dealt, raw):
+    nc.vector.tensor_copy(dealt.rearrange("p (t m) -> p t m", t=PACK), raw.rearrange("p (m t) -> p t m", t=PACK))
+
+
 def tile_picked_hpqgspangap_none_po_kernel(
     tc, x_words, x_scales, d_words, d_scales, gn, w1_words, w1_scales, offs, k1, n1, n2, n3, out_0, out_1, out_2
 ):
@@ -40,6 +50,7 @@ def tile_picked_hpqgspangap_none_po_kernel(
     with ExitStack() as ctx:
         lists = ctx.enter_context(tc.tile_pool(name="lists", bufs=1))
         keep = ctx.enter_context(tc.tile_pool(name="keep", bufs=1))
+        reused = ctx.enter_context(tc.tile_pool(name="reused", bufs=1))
         psum = ctx.enter_context(tc.psum_pool(name="psum", bufs=1))
 
         k1_list = lists.tile([P, H // 16], U16, name="k1_list")
@@ -49,7 +60,7 @@ def tile_picked_hpqgspangap_none_po_kernel(
         n3_list = lists.tile([P, S // 16], U16, name="n3_list")
 
         d_word_table = keep.tile([P, G], I32, name="d_word_table")
-        x_word_table = keep.tile([P, T], I32, name="x_word_table")
+        x_word_table = reused.tile([P, T], I32, name="x_word_table", offset=0, align_bytes=64)
         d_byte_table = keep.tile([P, G], U8, name="d_byte_table")
         x_byte_table = keep.tile([P, T], U8, name="x_byte_table")
         w1_raw_words = keep.tile([P, N], I32, name="w1_raw_words")
@@ -59,20 +70,19 @@ def tile_picked_hpqgspangap_none_po_kernel(
 
         nc.gpsimd.memset(d_byte_table[:].bitcast(I32), 0)
         nc.vector.memset(x_byte_table[:].bitcast(I32), 0)
+        nc.vector.memset(plane[:].bitcast(I32), 0)
+        nc.gpsimd.memset(w1_raw_bytes[:].bitcast(I32), 0)
         nc.sync.dma_start(k1_list[:], k1)
         nc.sync.dma_start(offs_list[:], offs)
         nc.sync.dma_start(n1_list[:], n1)
-        nc.sync.dma_start(n2_list[:], n2)
-        nc.sync.dma_start(n3_list[:], n3)
+        nc.sync.dma_start(gain[:], gn.rearrange("(p t) o -> p (t o)", t=PACK))
         nc.sync.dma_start(d_byte_table[:].bitcast(I32)[0:P:8, :], d_scales[0].bitcast(I32))
         nc.sync.dma_start(x_byte_table[:].bitcast(I32)[0:P:8, :], x_scales[0].bitcast(I32))
         nc.sync.dma_start(d_word_table[:], as_words(d_words))
         nc.sync.dma_start(x_word_table[:], as_words(x_words))
         nc.sync.dma_start(w1_raw_words[:], as_words(w1_words))
-
-        nc.gpsimd.dma_start(gain[:], gn.rearrange("(p t) o -> p (t o)", t=PACK))
-        nc.gpsimd.memset(plane[:].bitcast(I32), 0)
-        nc.gpsimd.memset(w1_raw_bytes[:].bitcast(I32), 0)
+        nc.sync.dma_start(n2_list[:], n2)
+        nc.sync.dma_start(n3_list[:], n3)
         for q in range(4):
             nc.gpsimd.dma_start(
                 w1_raw_bytes[:].bitcast(I32)[32 * q : 32 * q + 4, :], w1_scales[0].bitcast(I32)[4 * q : 4 * q + 4, :]
@@ -87,10 +97,7 @@ def tile_picked_hpqgspangap_none_po_kernel(
         x_picked_bytes = keep.tile([P, S], U8, name="x_picked_bytes")
         staged_bytes = keep.tile([P, S + H], U8, name="staged_bytes")
         nc.vector.tensor_copy(d_picked_bytes[:], d_byte_table[:].indirect(k1_list[:]))
-        nc.vector.tensor_copy(
-            staged_bytes[:, S:].rearrange("p (t m) -> p t m", t=PACK),
-            d_picked_bytes[:].rearrange("p (m t) -> p t m", t=PACK),
-        )
+        deal_bytes(nc, staged_bytes[:, S:], d_picked_bytes[:])
         nc.vector.tensor_copy(x_picked_bytes[:], x_byte_table[:].indirect(offs_list[:]))
         nc.vector.tensor_copy(staged_bytes[:].bitcast(I32)[:, : S // 4], x_picked_bytes[:].bitcast(I32))
         for c in range(4):
@@ -99,10 +106,7 @@ def tile_picked_hpqgspangap_none_po_kernel(
         d_picked_words = keep.tile([P, H], U32, name="d_picked_words")
         d_dealt_words = keep.tile([P, H], U32, name="d_dealt_words", align_bytes=64)
         nc.vector.tensor_copy(d_picked_words[:], d_word_table[:].bitcast(U32).indirect(k1_list[:]))
-        nc.vector.tensor_copy(
-            d_dealt_words[:].bitcast(I32).rearrange("p (t m) -> p t m", t=PACK),
-            d_picked_words[:].bitcast(I32).rearrange("p (m t) -> p t m", t=PACK),
-        )
+        deal_words(nc, d_dealt_words[:].bitcast(I32), d_picked_words[:].bitcast(I32))
 
         h_rows = [keep.tile([P, S], F32, name=f"h_rows{t}") for t in range(PACK)]
         for half in range(S // HALF):
@@ -111,6 +115,11 @@ def tile_picked_hpqgspangap_none_po_kernel(
             nc.vector.tensor_copy(
                 x_picked_words[:], x_word_table[:].bitcast(U32).indirect(entries(offs_list, cols.start, HALF))
             )
+            if half == 1:
+                w1_dealt_words = reused.tile([P, N], I32, name="w1_dealt_words", offset=0, align_bytes=64)
+                w1_dealt_bytes = reused.tile([P, N], U8, name="w1_dealt_bytes", offset=4 * N, align_bytes=64)
+                deal_words(nc, w1_dealt_words[:], w1_raw_words[:])
+                deal_bytes(nc, w1_dealt_bytes[:], w1_raw_bytes[:])
             for t in range(PACK):
                 bank = psum.tile([P, HALF], F32, name=f"h_bank{half}_{t}", tag=f"bank{PACK * half + t}")
                 nc.tensor.matmul_mx(
@@ -127,17 +136,6 @@ def tile_picked_hpqgspangap_none_po_kernel(
                 else:
                     nc.vector.tensor_scalar(h_rows[t][:, cols], bank[:], gain_size[:, t : t + 1], None, ALU.mult)
 
-        w1_dealt_words = keep.tile([P, N], I32, name="w1_dealt_words", align_bytes=64)
-        w1_dealt_bytes = keep.tile([P, N], U8, name="w1_dealt_bytes", align_bytes=64)
-        nc.gpsimd.tensor_copy(
-            w1_dealt_bytes[:].rearrange("p (t m) -> p t m", t=PACK),
-            w1_raw_bytes[:].rearrange("p (m t) -> p t m", t=PACK),
-        )
-        nc.gpsimd.tensor_copy(
-            w1_dealt_words[:].rearrange("p (t m) -> p t m", t=PACK),
-            w1_raw_words[:].rearrange("p (m t) -> p t m", t=PACK),
-        )
-
         units = S // UNIT
         members = [keep.tile([P, PACK, UNIT * MEMBERS], F32, name=f"members{u}") for u in range(units)]
         for u in range(units):
@@ -153,8 +151,8 @@ def tile_picked_hpqgspangap_none_po_kernel(
         early_banks = [psum.tile([P, early], F32, name=f"h2_early{t}", tag=f"bank{t}") for t in range(PACK)]
         late_banks = [psum.tile([P, CHUNK], F32, name=f"h2_late{t}", tag=f"bank{PACK + t}") for t in range(PACK)]
 
-        larger = keep.tile([P, S, PACK, 2], F32, name="larger")
-        smaller = keep.tile([P, S, PACK, 2], F32, name="smaller")
+        larger = keep.tile([P, S, 2, 2, 2], F32, name="larger")
+        smaller = keep.tile([P, S, 2, 2, 2], F32, name="smaller")
         largest = keep.tile([P, S * PACK], F32, name="largest")
         smallest = keep.tile([P, S * PACK], F32, name="smallest")
         z_size = keep.tile([P, S * PACK], BF16, name="z_size")
@@ -166,14 +164,19 @@ def tile_picked_hpqgspangap_none_po_kernel(
             return slice(cols.start * PACK, cols.stop * PACK)
 
         def pair_level(u, op, pairs):
-            halves = members[u][:].rearrange("p t (j a e) -> p j t a e", a=2, e=2)
+            halves = members[u][:].rearrange("p (a b) (j side e) -> p j a b side e", b=2, side=2, e=2)
             nc.vector.tensor_tensor(
-                pairs[:, u * UNIT : (u + 1) * UNIT, :, :], halves[:, :, :, 0, :], halves[:, :, :, 1, :], op
+                pairs[:, u * UNIT : (u + 1) * UNIT, :, :, :].rearrange("p j a e b -> p j a b e"),
+                halves[:, :, :, :, 0, :],
+                halves[:, :, :, :, 1, :],
+                op,
             )
 
         def last_level(cols, op, pairs, best):
-            both = pairs[:, cols, :, :].rearrange("p j t e -> p (j t) e")
-            nc.vector.tensor_tensor(best[:, flat(cols)], both[:, :, 0], both[:, :, 1], op)
+            both = pairs[:, cols, :, :, :].rearrange("p j a e b -> p (j a) e b")
+            nc.vector.tensor_tensor(
+                best[:, flat(cols)].rearrange("p (x b) -> p x b", b=2), both[:, :, 0, :], both[:, :, 1, :], op
+            )
 
         def combine(cols):
             nc.vector.scalar_tensor_tensor(
@@ -246,9 +249,11 @@ def tile_picked_hpqgspangap_none_po_kernel(
         taken = [keep.tile([P, PACK, HALF], F32, name=f"taken{half}") for half in range(S // HALF)]
         for half in range(S // HALF):
             for t in range(PACK):
-                nc.scalar.activation(
-                    taken[half][:, t, :], h2_rows[t][:].indirect(entries(n3_list, half * HALF, HALF)), ACT.Copy
-                )
+                looked_up = h2_rows[t][:].indirect(entries(n3_list, half * HALF, HALF))
+                if half == 0 and t == 1:
+                    nc.vector.tensor_copy(taken[half][:, t, :], looked_up)
+                else:
+                    nc.scalar.activation(taken[half][:, t, :], looked_up, ACT.Copy)
         ys = []
         for half in range(S // HALF):
             cols = slice(half * HALF, (half + 1) * HALF)

@@ -21,7 +21,8 @@ MEMBERS = 4
 HALF = 256
 CHUNK = 128
 UNIT = 64
-VECTOR_FETCHES = 2
+VECTOR_FETCHES = 3
+SCALAR_ROUNDS = 96
 
 
 def as_words(packed):
@@ -64,29 +65,25 @@ def tile_picked_hpqgspangap_none_po_kernel(
         d_byte_table = keep.tile([P, G], U8, name="d_byte_table")
         x_byte_table = keep.tile([P, T], U8, name="x_byte_table")
         w1_raw_words = keep.tile([P, N], I32, name="w1_raw_words")
-        w1_raw_bytes = keep.tile([P, N], U8, name="w1_raw_bytes")
         gain = keep.tile([P, PACK], F32, name="gain")
-        plane = keep.tile([P, S + H], U8, name="plane", align_bytes=64)
+        plane = keep.tile([P, S + H + N], U8, name="plane", align_bytes=64)
+        staged_bytes = keep.tile([P, S + H + N], U8, name="staged_bytes")
 
         nc.gpsimd.memset(d_byte_table[:].bitcast(I32), 0)
         nc.vector.memset(x_byte_table[:].bitcast(I32), 0)
         nc.vector.memset(plane[:].bitcast(I32), 0)
-        nc.gpsimd.memset(w1_raw_bytes[:].bitcast(I32), 0)
         nc.sync.dma_start(k1_list[:], k1)
         nc.sync.dma_start(offs_list[:], offs)
-        nc.sync.dma_start(n1_list[:], n1)
+        nc.sync.dma_start(staged_bytes[:, S + H :].bitcast(I32)[0:P:8, :], w1_scales[0].bitcast(I32))
         nc.sync.dma_start(gain[:], gn.rearrange("(p t) o -> p (t o)", t=PACK))
         nc.sync.dma_start(d_byte_table[:].bitcast(I32)[0:P:8, :], d_scales[0].bitcast(I32))
         nc.sync.dma_start(x_byte_table[:].bitcast(I32)[0:P:8, :], x_scales[0].bitcast(I32))
         nc.sync.dma_start(d_word_table[:], as_words(d_words))
+        nc.sync.dma_start(n1_list[:], n1)
         nc.sync.dma_start(x_word_table[:], as_words(x_words))
         nc.sync.dma_start(w1_raw_words[:], as_words(w1_words))
         nc.sync.dma_start(n2_list[:], n2)
         nc.sync.dma_start(n3_list[:], n3)
-        for q in range(4):
-            nc.gpsimd.dma_start(
-                w1_raw_bytes[:].bitcast(I32)[32 * q : 32 * q + 4, :], w1_scales[0].bitcast(I32)[4 * q : 4 * q + 4, :]
-            )
 
         gain_size = keep.tile([P, PACK], F32, name="gain_size")
         gain_sign = keep.tile([P, CHUNK, PACK], BF16, name="gain_sign")
@@ -95,9 +92,8 @@ def tile_picked_hpqgspangap_none_po_kernel(
 
         d_picked_bytes = keep.tile([P, H], U8, name="d_picked_bytes")
         x_picked_bytes = keep.tile([P, S], U8, name="x_picked_bytes")
-        staged_bytes = keep.tile([P, S + H], U8, name="staged_bytes")
         nc.vector.tensor_copy(d_picked_bytes[:], d_byte_table[:].indirect(k1_list[:]))
-        deal_bytes(nc, staged_bytes[:, S:], d_picked_bytes[:])
+        deal_bytes(nc, staged_bytes[:, S : S + H], d_picked_bytes[:])
         nc.vector.tensor_copy(x_picked_bytes[:], x_byte_table[:].indirect(offs_list[:]))
         nc.vector.tensor_copy(staged_bytes[:].bitcast(I32)[:, : S // 4], x_picked_bytes[:].bitcast(I32))
         for c in range(4):
@@ -109,32 +105,32 @@ def tile_picked_hpqgspangap_none_po_kernel(
         deal_words(nc, d_dealt_words[:].bitcast(I32), d_picked_words[:].bitcast(I32))
 
         h_rows = [keep.tile([P, S], F32, name=f"h_rows{t}") for t in range(PACK)]
-        for half in range(S // HALF):
-            cols = slice(half * HALF, (half + 1) * HALF)
-            x_picked_words = keep.tile([P, HALF], U32, name=f"x_picked_words{half}", align_bytes=64)
+        x_picked_words = keep.tile([P, S], U32, name="x_picked_words", align_bytes=64)
+        for first in (0, HALF):
             nc.vector.tensor_copy(
-                x_picked_words[:], x_word_table[:].bitcast(U32).indirect(entries(offs_list, cols.start, HALF))
+                x_picked_words[:, first : first + HALF],
+                x_word_table[:].bitcast(U32).indirect(entries(offs_list, first, HALF)),
             )
-            if half == 1:
-                w1_dealt_words = reused.tile([P, N], I32, name="w1_dealt_words", offset=0, align_bytes=64)
-                w1_dealt_bytes = reused.tile([P, N], U8, name="w1_dealt_bytes", offset=4 * N, align_bytes=64)
-                deal_words(nc, w1_dealt_words[:], w1_raw_words[:])
-                deal_bytes(nc, w1_dealt_bytes[:], w1_raw_bytes[:])
-            for t in range(PACK):
-                bank = psum.tile([P, HALF], F32, name=f"h_bank{half}_{t}", tag=f"bank{PACK * half + t}")
-                nc.tensor.matmul_mx(
-                    out=bank[:],
-                    lhsT=d_dealt_words[:, t * P : (t + 1) * P].bitcast(FP8X4),
-                    lhsT_scale=plane[:, S + t * P : S + (t + 1) * P],
-                    rhs=x_picked_words[:].bitcast(FP8X4),
-                    rhs_scale=plane[:, cols],
-                    start=True,
-                    stop=True,
-                )
-                if half == 0 or t == 0:
-                    nc.scalar.activation(h_rows[t][:, cols], bank[:], ACT.Copy, scale=gain_size[:, t : t + 1])
-                else:
-                    nc.vector.tensor_scalar(h_rows[t][:, cols], bank[:], gain_size[:, t : t + 1], None, ALU.mult)
+        w1_dealt_words = reused.tile([P, N], I32, name="w1_dealt_words", offset=0, align_bytes=64)
+        w1_dealt_bytes = reused.tile([P, N], U8, name="w1_dealt_bytes", offset=4 * N, align_bytes=64)
+        deal_words(nc, w1_dealt_words[:], w1_raw_words[:])
+        deal_bytes(nc, w1_dealt_bytes[:], plane[:, S + H :])
+        left, right, whole = slice(0, HALF), slice(HALF, S), slice(0, S)
+        for step, (t, cols) in enumerate([(0, left), (1, left), (0, right), (1, right), (2, whole), (3, whole)]):
+            bank = psum.tile([P, cols.stop - cols.start], F32, name=f"h_bank{step}", tag=f"bank{step}")
+            nc.tensor.matmul_mx(
+                out=bank[:],
+                lhsT=d_dealt_words[:, t * P : (t + 1) * P].bitcast(FP8X4),
+                lhsT_scale=plane[:, S + t * P : S + (t + 1) * P],
+                rhs=x_picked_words[:, cols].bitcast(FP8X4),
+                rhs_scale=plane[:, cols],
+                start=True,
+                stop=True,
+            )
+            if step < 3:
+                nc.scalar.activation(h_rows[t][:, cols], bank[:], ACT.Copy, scale=gain_size[:, t : t + 1])
+            else:
+                nc.vector.tensor_scalar(h_rows[t][:, cols], bank[:], gain_size[:, t : t + 1], None, ALU.mult)
 
         units = S // UNIT
         members = [keep.tile([P, PACK, UNIT * MEMBERS], F32, name=f"members{u}") for u in range(units)]
@@ -265,17 +261,21 @@ def tile_picked_hpqgspangap_none_po_kernel(
                     taken[half][:, t, :],
                     ALU.subtract,
                 )
-            nc.sync.dma_start(out_rows[:, :, cols], y[:])
+                if half == 1:
+                    nc.sync.dma_start(out_rows[:, t, cols], y[:, t, :])
+            if half == 0:
+                nc.sync.dma_start(out_rows[:, :, cols], y[:])
             ys.append(y)
         for half in range(S // HALF):
             cols = slice(half * HALF, (half + 1) * HALF)
             y_rounded = keep.tile([P, HALF, PACK], BF16, name=f"y_rounded{half}", align_bytes=64)
-            src = ys[half][:].rearrange("p t (c i) -> p c t i", i=4)
-            dst = y_rounded[:].rearrange("p (c i) t -> p c t i", i=4)
+            src = ys[half][:].rearrange("p t (c i) -> p c t i", i=2)
+            dst = y_rounded[:].rearrange("p (c i) t -> p c t i", i=2)
             if half == 0:
                 nc.scalar.copy(dst, src)
             else:
-                nc.vector.tensor_copy(dst, src)
+                nc.scalar.copy(dst[:, : SCALAR_ROUNDS // 2], src[:, : SCALAR_ROUNDS // 2])
+                nc.vector.tensor_copy(dst[:, SCALAR_ROUNDS // 2 :], src[:, SCALAR_ROUNDS // 2 :])
             y_words = keep.tile([P, HALF], U32, name=f"y_words{half}", align_bytes=64)
             nc.vector.quantize_mx(
                 out=y_words[:].bitcast(FP8X4), scales=y_bytes[:, cols], in_=y_rounded[:].rearrange("p j t -> p (j t)")

from contextlib import ExitStack

import concourse.mybir as mybir

K, T, S, N, G, H = 512, 2048, 512, 512, 2048, 512
FLOPS = 2 * K * H * S + 2 * H * N * S

F32 = mybir.dt.float32
BF16 = mybir.dt.bfloat16
I32 = mybir.dt.int32
U32 = mybir.dt.uint32
U16 = mybir.dt.uint16
U8 = mybir.dt.uint8
FP8X4 = mybir.dt.float8_e4m3fn_x4
ALU = mybir.AluOpType
ACT = mybir.ActivationFunctionType

P = 128
PACK = 4
MEMBERS = 4
HALF = 256
CHUNK = 128
UNIT = 64
VECTOR_FETCHES = 3
SCALAR_ROUNDS = 96


def as_words(packed):
    return packed[0].rearrange("p n t -> p (n t)").bitcast(I32)


def entries(list_tile, first, count):
    return list_tile[:, first // 16 : (first + count) // 16]


def deal_words(nc, dealt, raw):
    nc.vector.tensor_copy(
        dealt.rearrange("p (t c i) -> p c t i", t=PACK, i=4), raw.rearrange("p (c i t) -> p c t i", t=PACK, i=4)
    )


def deal_bytes(nc, dealt, raw):
    nc.vector.tensor_copy(dealt.rearrange("p (t m) -> p t m", t=PACK), raw.rearrange("p (m t) -> p t m", t=PACK))


def tile_picked_hpqgspangap_none_po_kernel(
    tc, x_words, x_scales, d_words, d_scales, gn, w1_words, w1_scales, offs, k1, n1, n2, n3, out_0, out_1, out_2
):
    nc = tc.nc
    chunks = S // CHUNK
    with ExitStack() as ctx:
        lists = ctx.enter_context(tc.tile_pool(name="lists", bufs=1))
        keep = ctx.enter_context(tc.tile_pool(name="keep", bufs=1))
        reused = ctx.enter_context(tc.tile_pool(name="reused", bufs=1))
        psum = ctx.enter_context(tc.psum_pool(name="psum", bufs=1))

        k1_list = lists.tile([P, H // 16], U16, name="k1_list")
        offs_list = lists.tile([P, S // 16], U16, name="offs_list")
        n1_list = lists.tile([P, G // 16], U16, name="n1_list")
        n2_list = lists.tile([P, S // 16], U16, name="n2_list")
        n3_list = lists.tile([P, S // 16], U16, name="n3_list")

        d_word_table = keep.tile([P, G], I32, name="d_word_table")
        x_word_table = reused.tile([P, T], I32, name="x_word_table", offset=0, align_bytes=64)
        d_byte_table = keep.tile([P, G], U8, name="d_byte_table")
        x_byte_table = keep.tile([P, T], U8, name="x_byte_table")
        w1_raw_words = keep.tile([P, N], I32, name="w1_raw_words")
        gain = keep.tile([P, PACK], F32, name="gain")
        plane = keep.tile([P, S + H + N], U8, name="plane", align_bytes=64)
        staged_bytes = keep.tile([P, S + H + N], U8, name="staged_bytes")

        nc.gpsimd.memset(d_byte_table[:].bitcast(I32), 0)
        nc.vector.memset(x_byte_table[:].bitcast(I32), 0)
        nc.vector.memset(plane[:].bitcast(I32), 0)
        nc.sync.dma_start(k1_list[:], k1)
        nc.sync.dma_start(offs_list[:], offs)
        nc.sync.dma_start(staged_bytes[:, S + H :].bitcast(I32)[0:P:8, :], w1_scales[0].bitcast(I32))
        nc.sync.dma_start(gain[:], gn.rearrange("(p t) o -> p (t o)", t=PACK))
        nc.sync.dma_start(d_byte_table[:].bitcast(I32)[0:P:8, :], d_scales[0].bitcast(I32))
        nc.sync.dma_start(x_byte_table[:].bitcast(I32)[0:P:8, :], x_scales[0].bitcast(I32))
        nc.sync.dma_start(d_word_table[:], as_words(d_words))
        nc.sync.dma_start(n1_list[:], n1)
        nc.sync.dma_start(x_word_table[:], as_words(x_words))
        nc.sync.dma_start(w1_raw_words[:], as_words(w1_words))
        nc.sync.dma_start(n2_list[:], n2)
        nc.sync.dma_start(n3_list[:], n3)

        gain_size = keep.tile([P, PACK], F32, name="gain_size")
        gain_sign = keep.tile([P, CHUNK, PACK], BF16, name="gain_sign")
        nc.scalar.activation(gain_size[:], gain[:], ACT.Abs, scale=0.0625)
        nc.scalar.activation(gain_sign[:], gain[:].unsqueeze(1).broadcast_to([P, CHUNK, PACK]), ACT.Sign)

        d_picked_bytes = keep.tile([P, H], U8, name="d_picked_bytes")
        x_picked_bytes = keep.tile([P, S], U8, name="x_picked_bytes")
        nc.vector.tensor_copy(d_picked_bytes[:], d_byte_table[:].indirect(k1_list[:]))
        deal_bytes(nc, staged_bytes[:, S : S + H], d_picked_bytes[:])
        nc.vector.tensor_copy(x_picked_bytes[:], x_byte_table[:].indirect(offs_list[:]))
        nc.vector.tensor_copy(staged_bytes[:].bitcast(I32)[:, : S // 4], x_picked_bytes[:].bitcast(I32))
        for c in range(4):
            nc.scalar.dma_start(plane[:].bitcast(I32)[c:P:32, :], staged_bytes[:].bitcast(I32)[8 * c : P : 32, :])

        d_picked_words = keep.tile([P, H], U32, name="d_picked_words")
        d_dealt_words = keep.tile([P, H], U32, name="d_dealt_words", align_bytes=64)
        nc.vector.tensor_copy(d_picked_words[:], d_word_table[:].bitcast(U32).indirect(k1_list[:]))
        deal_words(nc, d_dealt_words[:].bitcast(I32), d_picked_words[:].bitcast(I32))

        h_rows = [keep.tile([P, S], F32, name=f"h_rows{t}") for t in range(PACK)]
        x_picked_words = keep.tile([P, S], U32, name="x_picked_words", align_bytes=64)
        for first in (0, HALF):
            nc.vector.tensor_copy(
                x_picked_words[:, first : first + HALF],
                x_word_table[:].bitcast(U32).indirect(entries(offs_list, first, HALF)),
            )
        w1_dealt_words = reused.tile([P, N], I32, name="w1_dealt_words", offset=0, align_bytes=64)
        w1_dealt_bytes = reused.tile([P, N], U8, name="w1_dealt_bytes", offset=4 * N, align_bytes=64)
        deal_words(nc, w1_dealt_words[:], w1_raw_words[:])
        deal_bytes(nc, w1_dealt_bytes[:], plane[:, S + H :])
        left, right, whole = slice(0, HALF), slice(HALF, S), slice(0, S)
        for step, (t, cols) in enumerate([(0, left), (1, left), (0, right), (1, right), (2, whole), (3, whole)]):
            bank = psum.tile([P, cols.stop - cols.start], F32, name=f"h_bank{step}", tag=f"bank{step}")
            nc.tensor.matmul_mx(
                out=bank[:],
                lhsT=d_dealt_words[:, t * P : (t + 1) * P].bitcast(FP8X4),
                lhsT_scale=plane[:, S + t * P : S + (t + 1) * P],
                rhs=x_picked_words[:, cols].bitcast(FP8X4),
                rhs_scale=plane[:, cols],
                start=True,
                stop=True,
            )
            if step < 3:
                nc.scalar.activation(h_rows[t][:, cols], bank[:], ACT.Copy, scale=gain_size[:, t : t + 1])
            else:
                nc.vector.tensor_scalar(h_rows[t][:, cols], bank[:], gain_size[:, t : t + 1], None, ALU.mult)

        units = S // UNIT
        members = [keep.tile([P, PACK, UNIT * MEMBERS], F32, name=f"members{u}") for u in range(units)]
        for u in range(units):
            for t in range(PACK):
                looked_up = h_rows[t][:].indirect(entries(n1_list, u * UNIT * MEMBERS, UNIT * MEMBERS))
                if u < VECTOR_FETCHES and t == PACK - 1:
                    nc.vector.tensor_copy(members[u][:, t, :], looked_up)
                else:
                    nc.scalar.activation(members[u][:, t, :], looked_up, ACT.Copy)

        h2_rows = [keep.tile([P, S], F32, name=f"h2_rows{t}") for t in range(PACK)]
        early = (chunks - 1) * CHUNK
        early_banks = [psum.tile([P, early], F32, name=f"h2_early{t}", tag=f"bank{t}") for t in range(PACK)]
        late_banks = [psum.tile([P, CHUNK], F32, name=f"h2_late{t}", tag=f"bank{PACK + t}") for t in range(PACK)]

        larger = keep.tile([P, S, 2, 2, 2], F32, name="larger")
        smaller = keep.tile([P, S, 2, 2, 2], F32, name="smaller")
        largest = keep.tile([P, S * PACK], F32, name="largest")
        smallest = keep.tile([P, S * PACK], F32, name="smallest")
        z_size = keep.tile([P, S * PACK], BF16, name="z_size")
        z = keep.tile([P, S * PACK], BF16, name="z", align_bytes=64)
        z_words = keep.tile([P, S], U32, name="z_words", align_bytes=64)
        z_bytes = keep.tile([P, S], U8, name="z_bytes", align_bytes=64)

        def flat(cols):
            return slice(cols.start * PACK, cols.stop * PACK)

        def pair_level(u, op, pairs):
            halves = members[u][:].rearrange("p (a b) (j side e) -> p j a b side e", b=2, side=2, e=2)
            nc.vector.tensor_tensor(
                pairs[:, u * UNIT : (u + 1) * UNIT, :, :, :].rearrange("p j a e b -> p j a b e"),
                halves[:, :, :, :, 0, :],
                halves[:, :, :, :, 1, :],
                op,
            )

        def last_level(cols, op, pairs, best):
            both = pairs[:, cols, :, :, :].rearrange("p j a e b -> p (j a) e b")
            nc.vector.tensor_tensor(
                best[:, flat(cols)].rearrange("p (x b) -> p x b", b=2), both[:, :, 0, :], both[:, :, 1, :], op
            )

        def combine(cols):
            nc.vector.scalar_tensor_tensor(
                z_size[:, flat(cols)], smallest[:, flat(cols)], -0.5, largest[:, flat(cols)], ALU.mult, ALU.add
            )

        def give_sign(cols):
            signs = gain_sign[:, : cols.stop - cols.start, :].rearrange("p j t -> p (j t)")
            nc.vector.tensor_tensor(z[:, flat(cols)], z_size[:, flat(cols)], signs, ALU.mult)

        def quantise(cols):
            nc.vector.quantize_mx(out=z_words[:, cols].bitcast(FP8X4), scales=z_bytes[:, cols], in_=z[:, flat(cols)])

        def second_product(cols, banks, bank_cols):
            for t in range(PACK):
                nc.tensor.matmul_mx(
                    out=banks[t][:, bank_cols],
                    lhsT=w1_dealt_words[:, t * P : (t + 1) * P].bitcast(FP8X4),
                    lhsT_scale=w1_dealt_bytes[:, t * P : (t + 1) * P],
                    rhs=z_words[:, cols].bitcast(FP8X4),
                    rhs_scale=z_bytes[:, cols],
                    start=True,
                    stop=True,
                )

        for c in range(chunks):
            first, second = 2 * c, 2 * c + 1
            cols = slice(c * CHUNK, (c + 1) * CHUNK)
            before = slice(cols.start - CHUNK, cols.start)
            first_cols = slice(cols.start, cols.start + UNIT)
            second_cols = slice(cols.start + UNIT, cols.stop)
            last = c == chunks - 1
            pair_level(first, ALU.max, larger)
            if c > 0:
                combine(before)
            pair_level(first, ALU.min, smaller)
            if c > 0:
                give_sign(before)
            if last:
                last_level(first_cols, ALU.max, larger, largest)
                quantise(before)
                second_product(before, early_banks, before)
                last_level(first_cols, ALU.min, smaller, smallest)
                for t in range(PACK):
                    nc.scalar.activation(h2_rows[t][:, :early], early_banks[t][:], ACT.Copy)
                pair_level(second, ALU.max, larger)
                pair_level(second, ALU.min, smaller)
                last_level(second_cols, ALU.max, larger, largest)
                last_level(second_cols, ALU.min, smaller, smallest)
                for step in (combine, give_sign, quantise):
                    step(first_cols)
                    step(second_cols)
                second_product(cols, late_banks, slice(0, CHUNK))
            else:
                pair_level(second, ALU.max, larger)
                if c > 0:
                    quantise(before)
                    second_product(before, early_banks, before)
                pair_level(second, ALU.min, smaller)
                last_level(cols, ALU.max, larger, largest)
                last_level(cols, ALU.min, smaller, smallest)
        for t in range(PACK):
            if t % 2 == 0:
                nc.scalar.activation(h2_rows[t][:, early:], late_banks[t][:], ACT.Copy)
            else:
                nc.vector.tensor_copy(h2_rows[t][:, early:], late_banks[t][:])

        out_rows = out_0.rearrange("(p t) j -> p t j", t=PACK)
        y_bytes = keep.tile([P, S], U8, name="y_bytes", align_bytes=64)
        taken = [keep.tile([P, PACK, HALF], F32, name=f"taken{half}") for half in range(S // HALF)]
        for half in range(S // HALF):
            for t in range(PACK):
                looked_up = h2_rows[t][:].indirect(entries(n3_list, half * HALF, HALF))
                if half == 0 and t == 1:
                    nc.vector.tensor_copy(taken[half][:, t, :], looked_up)
                else:
                    nc.scalar.activation(taken[half][:, t, :], looked_up, ACT.Copy)
        ys = []
        for half in range(S // HALF):
            cols = slice(half * HALF, (half + 1) * HALF)
            y = keep.tile([P, PACK, HALF], F32, name=f"y{half}")
            for t in range(PACK):
                nc.vector.tensor_tensor(
                    y[:, t, :],
                    h2_rows[t][:].indirect(entries(n2_list, cols.start, HALF)),
                    taken[half][:, t, :],
                    ALU.subtract,
                )
                if half == 1:
                    nc.sync.dma_start(out_rows[:, t, cols], y[:, t, :])
            if half == 0:
                nc.sync.dma_start(out_rows[:, :, cols], y[:])
            ys.append(y)
        for half in range(S // HALF):
            cols = slice(half * HALF, (half + 1) * HALF)
            y_rounded = keep.tile([P, HALF, PACK], BF16, name=f"y_rounded{half}", align_bytes=64)
            src = ys[half][:].rearrange("p t (c i) -> p c t i", i=2)
            dst = y_rounded[:].rearrange("p (c i) t -> p c t i", i=2)
            if half == 0:
                nc.scalar.copy(dst, src)
            else:
                nc.scalar.copy(dst[:, : SCALAR_ROUNDS // 2], src[:, : SCALAR_ROUNDS // 2])
                nc.vector.tensor_copy(dst[:, SCALAR_ROUNDS // 2 :], src[:, SCALAR_ROUNDS // 2 :])
            y_words = keep.tile([P, HALF], U32, name=f"y_words{half}", align_bytes=64)
            nc.vector.quantize_mx(
                out=y_words[:].bitcast(FP8X4), scales=y_bytes[:, cols], in_=y_rounded[:].rearrange("p j t -> p (j t)")
            )
            nc.sync.dma_start(as_words(out_1)[:, cols], y_words[:].bitcast(I32))
        for q in range(4):
            queue = nc.scalar if q % 2 == 0 else nc.sync
            queue.dma_start(
                out_2[0].bitcast(I32)[4 * q : 4 * q + 4, :], y_bytes[:].bitcast(I32)[32 * q : 32 * q + 4, :]
            )
